import numpy as np
import ml_dtypes


def mxq(x, axis, fmt="e4m3"):
    dtype, down = {"e4m3": (ml_dtypes.float8_e4m3fn, 7), "e5m2": (ml_dtypes.float8_e5m2, 14)}[fmt]
    v = np.moveaxis(np.asarray(x, np.float32).astype(ml_dtypes.bfloat16).astype(np.float64), axis, -1)
    blocks = v.reshape(v.shape[:-1] + (-1, 32))
    amax = np.abs(blocks).max(-1, keepdims=True)
    byte = np.maximum(np.where(amax > 0, np.frexp(amax)[1] - 1 + 127, 0) - down, 1)
    scale = np.exp2(byte - 127.0)
    codes = (blocks / scale).astype(np.float32).astype(dtype).astype(np.float64)
    return np.moveaxis((codes * scale).reshape(v.shape), -1, axis)


WIDE = False


def mx_kscale(k):
    if not WIDE:
        return np.ones(k)
    levels = np.array([10, -10, 5, -5, 0])
    if k % 512:
        return np.exp2(np.random.permutation(np.resize(levels, k // 32))).repeat(32)
    a = np.empty((k // 512, 16))
    for p in range(k // 512):
        a[p, :8] = np.random.permutation(np.resize(levels, 8))
        for g in range(8):
            far = levels[np.abs(levels - a[p, g]) >= 10]
            a[p, g + 8] = far[np.random.randint(len(far))]
    return np.exp2(a.ravel()).repeat(32)


BF16 = ml_dtypes.bfloat16


def bf(x):
    return np.asarray(x, np.float32).astype(BF16)


def f64(x):
    return np.asarray(x).astype(np.float64)

def planes(Y):
    n, m = Y.shape
    b = f64(bf(Y)).reshape(n // 32, 32, m)
    amax = np.abs(b).max(1)
    byte = np.clip(np.where(amax > 0, np.frexp(amax)[1] - 1 + 127 - 7, 1), 1, 254)
    codes = (b * np.exp2(127.0 - byte)[:, None, :]).reshape(n, m).astype(np.float32).astype(ml_dtypes.float8_e4m3fn).view(np.uint8)
    words = codes.reshape(n // 512, 128, 4, m).transpose(0, 1, 3, 2)
    return np.ascontiguousarray(words), np.ascontiguousarray(byte.astype(np.uint8).reshape(n // 512, 16, m))


M, N, D, V = 3, 256, 1024, 2048

EPS = 0.001
DELTA = 0.3
SPREAD = 0.65 * np.sqrt(2.0 * (np.log(V) - np.log(DELTA / EPS)))


def setup_inputs():
    s, t = mx_kscale(D), mx_kscale(D)
    return {
        "h": bf(np.random.standard_normal((N, D)) * s),
        "w_res": bf(np.random.standard_normal((M, D, D)) * 1.5 / np.sqrt(D) / s[None, :, None]),
        "a_skip": bf((1.0 + 0.25 * np.random.standard_normal((M, D))) * (t / s)),
        "g_silu": bf((1.0 + 0.25 * np.random.standard_normal((M, D))) * t),
        "w_head": bf(np.random.standard_normal((M, D, V)) * SPREAD / np.sqrt(D) / t[None, :, None]),
        "temp": bf(np.random.uniform(0.5, 1.5, N)),
    }


def stable_log_softmax(z):
    z_max = np.max(z, axis=-1, keepdims=True)
    lse = z_max + np.log(np.sum(np.exp(z - z_max), axis=-1, keepdims=True))
    return z - lse


def stable_softplus(x):
    return np.maximum(x, 0.0) + np.log(1.0 + np.exp(-np.abs(x)))


def sigmoid(x):
    return 1.0 / (1.0 + np.exp(-x))


def core(h, w_res, a_skip, g_silu, w_head, temp):
    h, a_skip, g_silu, temp = f64(h), f64(a_skip), f64(g_silu), f64(temp)

    u = mxq(h, 1, "e4m3") @ mxq(f64(w_res), 1, "e4m3")

    r = a_skip[:, None, :] * h[None, :, :] + g_silu[:, None, :] * u * sigmoid(u)

    z = (mxq(r, 2, "e4m3") @ mxq(f64(w_head), 1, "e4m3")) / temp[None, :, None]

    logp = stable_log_softmax(z)

    ent = -np.sum(np.exp(logp) * logp, axis=-1)

    thr = np.minimum(np.log(EPS), np.log(DELTA) - ent)

    return -stable_softplus(-(logp - thr[:, :, None]) / 2.0)


def reference(h, w_res, a_skip, g_silu, w_head, temp):
    R_out = core(h, w_res, a_skip, g_silu, w_head, temp)
    words, scales = planes(np.moveaxis(R_out, 2, 0).reshape(2048, -1))
    return R_out, words, scales

import math
from contextlib import ExitStack

import concourse.mybir as mybir
from concourse.masks import make_identity

HEADS, N, D, V = 3, 256, 1024, 2048
FLOPS = 2 * HEADS * N * D * (D + V)

F32 = mybir.dt.float32
BF16 = mybir.dt.bfloat16
U32 = mybir.dt.uint32
I32 = mybir.dt.int32
U8 = mybir.dt.uint8
FP8X4 = mybir.dt.float8_e4m3fn_x4
ACT = mybir.ActivationFunctionType
ALU = mybir.AluOpType

P = 128
J = 4
EPS, DELTA = 0.001, 0.3
RAW_BUFS = 4
RES_CHUNKS = 12
CHUNKS = 36
S_RES = (1, 3, 5)
S_HEAD = (1, 3, 5, 7)
S_EXTRA = (17, 30)
V_SQUARES = (4, 5)
S_TURN = (0, 2, 3)
S_DIAGS = ()
H_SCALAR = False
PB = 3

ORDER = [
    ("interleave", (0, )),
    ("interleave", (1, )),
    ("quantize", (0, )),
    ("params", ()),
    ("scales2", ()),
    ("diags", (1, 0, 0, False, )),
    ("diags", (1, 0, 1, False, )),
    ("diags", (1, 0, 2, False, )),
    ("diags", (1, 0, 3, False, )),
    ("diags", (1, 1, 0, False, )),
    ("diags", (1, 1, 1, False, )),
    ("diags", (1, 1, 2, False, )),
    ("prepare_h", (0, )),
    ("diags", (0, 0, 0, True, )),
    ("quantize", (1, )),
    ("diags", (0, 0, 1, True, )),
    ("diags", (0, 0, 2, True, )),
    ("prepare_h", (1, )),
    ("diags", (0, 0, 3, True, )),
    ("diags", (0, 1, 0, True, )),
    ("interleave", (2, )),
    ("diags", (0, 1, 1, True, )),
    ("diags", (0, 1, 2, True, )),
    ("diags", (0, 1, 3, True, )),
    ("quantize_h", (0, )),
    ("interleave", (3, )),
    ("quantize", (2, )),
    ("interleave", (4, )),
    ("quantize_h", (1, )),
    ("interleave", (5, )),
    ("quantize", (3, )),
    ("stage1", (0, 0, 0, )),
    ("stage1", (0, 0, 1, )),
    ("quantize", (4, )),
    ("stage1", (0, 1, 0, )),
    ("interleave", (6, )),
    ("stage1", (0, 1, 1, )),
    ("silu", (0, 0, 0, )),
    ("diags", (1, 1, 3, False, )),
    ("interleave", (7, )),
    ("silu", (0, 0, 1, )),
    ("silu", (0, 1, 0, )),
    ("quantize", (5, )),
    ("silu", (0, 1, 1, )),
    ("mix", (0, 0, 0, )),
    ("diags", (2, 0, 0, False, )),
    ("mix_out", (0, 0, 0, )),
    ("diags", (2, 0, 1, False, )),
    ("diags", (2, 0, 2, False, )),
    ("diags", (2, 0, 3, False, )),
    ("diags", (2, 1, 0, False, )),
    ("mix", (0, 0, 1, )),
    ("diags", (2, 1, 1, False, )),
    ("diags", (2, 1, 2, False, )),
    ("diags", (2, 1, 3, False, )),
    ("interleave", (8, )),
    ("mix_out", (0, 0, 1, )),
    ("mix", (0, 1, 0, )),
    ("quantize", (6, )),
    ("mix_out", (0, 1, 0, )),
    ("quantize_r", (0, 0, )),
    ("interleave", (13, )),
    ("interleave", (9, )),
    ("mix", (0, 1, 1, )),
    ("stage1", (1, 0, 0, )),
    ("quantize", (7, )),
    ("stage1", (1, 0, 1, )),
    ("interleave", (10, )),
    ("stage1", (1, 1, 0, )),
    ("mix_out", (0, 1, 1, )),
    ("stage1", (1, 1, 1, )),
    ("silu", (1, 0, 0, )),
    ("quantize_r", (0, 1, )),
    ("quantize", (8, )),
    ("silu", (1, 0, 1, )),
    ("interleave", (11, )),
    ("silu", (1, 1, 0, )),
    ("mix", (1, 0, 0, )),
    ("silu", (1, 1, 1, )),
    ("quantize", (9, )),
    ("mix_out", (1, 0, 0, )),
    ("interleave", (12, )),
    ("mix", (1, 0, 1, )),
    ("interleave", (15, )),
    ("quantize", (10, )),
    ("mix", (1, 1, 0, )),
    ("quantize", (11, )),
    ("interleave", (14, )),
    ("mix_out", (1, 0, 1, )),
    ("mix_out", (1, 1, 0, )),
    ("mix", (1, 1, 1, )),
    ("quantize_r", (1, 0, )),
    ("mix_out", (1, 1, 1, )),
    ("stage1", (2, 0, 0, )),
    ("quantize", (12, )),
    ("silu", (2, 0, 0, )),
    ("stage1", (2, 0, 1, )),
    ("quantize_r", (1, 1, )),
    ("quantize", (13, )),
    ("silu", (2, 0, 1, )),
    ("stage1", (2, 1, 0, )),
    ("interleave", (16, )),
    ("silu", (2, 1, 0, )),
    ("stage1", (2, 1, 1, )),
    ("silu", (2, 1, 1, )),
    ("quantize", (14, )),
    ("interleave", (17, )),
    ("mix", (2, 0, 0, )),
    ("quantize", (15, )),
    ("interleave", (18, )),
    ("mix", (2, 0, 1, )),
    ("mix_out", (2, 0, 0, )),
    ("quantize", (16, )),
    ("mix_out", (2, 0, 1, )),
    ("quantize", (17, )),
    ("interleave", (19, )),
    ("mix", (2, 1, 0, )),
    ("quantize_r", (2, 0, )),
    ("interleave", (20, )),
    ("quantize", (18, )),
    ("mix", (2, 1, 1, )),
    ("mix_out", (2, 1, 0, )),
    ("interleave", (22, )),
    ("logits", (0, 0, 0, )),
    ("mix_out", (2, 1, 1, )),
    ("logits", (0, 0, 1, )),
    ("scale_max", (0, 0, 0, )),
    ("interleave", (21, )),
    ("logits", (0, 1, 0, )),
    ("logits", (0, 1, 1, )),
    ("quantize_r", (2, 1, )),
    ("scale_max", (0, 0, 1, )),
    ("logits", (0, 2, 0, )),
    ("scale_max", (0, 1, 0, )),
    ("logits", (0, 2, 1, )),
    ("interleave", (23, )),
    ("scale_max", (0, 1, 1, )),
    ("quantize", (19, )),
    ("scale_max", (0, 2, 0, )),
    ("logits", (0, 3, 0, )),
    ("logits", (0, 3, 1, )),
    ("scale_max", (0, 2, 1, )),
    ("interleave", (25, )),
    ("quantize", (20, )),
    ("scale_max", (0, 3, 0, )),
    ("scale_max", (0, 3, 1, )),
    ("interleave", (27, )),
    ("row_max", (0, )),
    ("quantize", (21, )),
    ("interleave", (24, )),
    ("expo", (0, )),
    ("quantize", (22, )),
    ("quantize", (23, )),
    ("logits", (1, 0, 0, )),
    ("logits", (1, 0, 1, )),
    ("interleave", (26, )),
    ("logits", (1, 1, 0, )),
    ("logits", (1, 1, 1, )),
    ("scale_max", (1, 0, 0, )),
    ("quantize", (24, )),
    ("scale_max", (1, 0, 1, )),
    ("square", (0, )),
    ("scale_max", (1, 1, 0, )),
    ("quantize", (25, )),
    ("scale_max", (1, 1, 1, )),
    ("interleave", (28, )),
    ("expo", (1, )),
    ("tpass", (0, )),
    ("interleave", (29, )),
    ("quantize", (26, )),
    ("quantize", (27, )),
    ("logits", (1, 2, 0, )),
    ("square", (1, )),
    ("logits", (1, 2, 1, )),
    ("quantize", (28, )),
    ("logits", (1, 3, 0, )),
    ("logits", (1, 3, 1, )),
    ("scale_max", (1, 2, 0, )),
    ("scale_max", (1, 2, 1, )),
    ("scale_max", (1, 3, 0, )),
    ("interleave", (30, )),
    ("tpass", (1, )),
    ("interleave", (31, )),
    ("kappa", (0, )),
    ("scale_max", (1, 3, 1, )),
    ("row_max", (1, )),
    ("quantize", (29, )),
    ("interleave", (32, )),
    ("interleave", (33, )),
    ("quantize", (30, )),
    ("quantize", (31, )),
    ("logits", (2, 0, 0, )),
    ("expo", (2, )),
    ("logits", (2, 0, 1, )),
    ("interleave", (34, )),
    ("logits", (2, 1, 0, )),
    ("logits", (2, 1, 1, )),
    ("scale_max", (2, 0, 0, )),
    ("scale_max", (2, 0, 1, )),
    ("expo", (3, )),
    ("quantize", (32, )),
    ("scale_max", (2, 1, 0, )),
    ("quantize", (33, )),
    ("scale_max", (2, 1, 1, )),
    ("square", (2, )),
    ("quantize", (34, )),
    ("logits", (2, 2, 0, )),
    ("logits", (2, 2, 1, )),
    ("scale_max", (2, 2, 0, )),
    ("interleave", (35, )),
    ("tpass", (2, )),
    ("quantize", (35, )),
    ("square", (3, )),
    ("scale_max", (2, 2, 1, )),
    ("logits", (2, 3, 0, )),
    ("logits", (2, 3, 1, )),
    ("scale_max", (2, 3, 0, )),
    ("scale_max", (2, 3, 1, )),
    ("tpass", (3, )),
    ("kappa", (1, )),
    ("row_max", (2, )),
    ("expo", (4, )),
    ("expo", (5, )),
    ("square", (4, )),
    ("ln", (0, None, )),
    ("tpass", (4, )),
    ("square", (5, )),
    ("ln", (1, None, )),
    ("tpass", (5, )),
    ("ln", (2, None, )),
    ("kappa", (2, )),
    ("final", (0, None, )),
    ("ln", (3, None, )),
    ("final", (1, None, )),
    ("turn", (0, 0, )),
    ("turn_out", (0, 0, True, )),
    ("turn", (0, 1, )),
    ("ln", (4, None, )),
    ("turn", (0, 2, )),
    ("turn", (0, 3, )),
    ("turn_out", (0, 1, False, )),
    ("turn", (1, 0, )),
    ("final", (2, None, )),
    ("turn", (1, 1, )),
    ("turn_out", (0, 2, True, )),
    ("turn", (1, 2, )),
    ("turn_out", (0, 3, True, )),
    ("turn", (1, 3, )),
    ("turn_out", (1, 0, True, )),
    ("planes", (0, None, )),
    ("turn_out", (1, 2, True, )),
    ("turn", (2, 0, )),
    ("turn_out", (1, 1, False, )),
    ("turn_out", (1, 3, True, )),
    ("turn", (2, 1, )),
    ("final", (3, None, )),
    ("turn_out", (2, 0, True, )),
    ("turn", (2, 2, )),
    ("turn_out", (2, 2, True, )),
    ("turn", (2, 3, )),
    ("turn_out", (2, 3, True, )),
    ("ln", (5, 0, )),
    ("planes", (1, None, )),
    ("ln", (5, 1, )),
    ("turn", (3, 0, )),
    ("turn_out", (2, 1, False, )),
    ("turn_out", (3, 0, True, )),
    ("turn", (3, 1, )),
    ("planes", (2, None, )),
    ("ln", (5, 2, )),
    ("turn", (3, 2, )),
    ("turn_out", (3, 1, False, )),
    ("turn_out", (3, 2, True, )),
    ("turn", (3, 3, )),
    ("final", (4, None, )),
    ("turn_out", (3, 3, True, )),
    ("ln", (5, 3, )),
    ("planes", (3, None, )),
    ("turn", (4, 0, )),
    ("final", (5, 0, )),
    ("turn_out", (4, 0, True, )),
    ("turn", (4, 1, )),
    ("final", (5, 1, )),
    ("turn", (4, 2, )),
    ("turn_out", (4, 1, False, )),
    ("turn_out", (4, 2, True, )),
    ("turn", (4, 3, )),
    ("final", (5, 2, )),
    ("turn_out", (4, 3, True, )),
    ("turn", (5, 0, )),
    ("final", (5, 3, )),
    ("turn_out", (5, 0, True, )),
    ("turn", (5, 1, )),
    ("planes", (4, None, )),
    ("turn", (5, 2, )),
    ("planes", (5, 0, )),
    ("turn_out", (5, 1, False, )),
    ("turn_out", (5, 2, True, )),
    ("turn", (5, 3, )),
    ("planes", (5, 1, )),
    ("planes", (5, 2, )),
    ("turn_out", (5, 3, False, )),
    ("planes", (5, 3, )),
]


def tile_medusatypicalacceptanceheads_x1_kernel(tc, h, w_res, a_skip, g_silu, w_head, temp, out_0, out_1, out_2):
    nc = tc.nc
    words = out_1.bitcast(I32).rearrange("g p m o -> p g (m o)")
    scale_rows = out_2.bitcast(I32)

    with ExitStack() as ctx:
        const = ctx.enter_context(tc.tile_pool(name="const", bufs=1))
        raws = ctx.enter_context(tc.tile_pool(name="raws", bufs=RAW_BUFS))
        mids = ctx.enter_context(tc.tile_pool(name="mids", bufs=5))
        codes = ctx.enter_context(tc.tile_pool(name="codes", bufs=12))
        units = ctx.enter_context(tc.tile_pool(name="units", bufs=6))
        work = ctx.enter_context(tc.tile_pool(name="work", bufs=2))
        pm = ctx.enter_context(tc.psum_pool(name="pm", bufs=5))
        pt = ctx.enter_context(tc.psum_pool(name="pt", bufs=3))

        ctx.enter_context(tc.manual_schedule())
        raw_tiles, mid_tiles, code_tiles = {}, {}, {}

        def place(c):
            k, part = divmod(c, 2)
            if c < RES_CHUNKS:
                m, g = divmod(k, 2)
                return "r", m, g, part
            m, rest = divmod(k - 6, 4)
            half, g = divmod(rest, 2)
            return "h", m, g, 2 * half + part

        def load(k):
            if k >= CHUNKS // 2:
                return
            raw = raws.tile([P, J, 1024], BF16, name="raw")
            kind, m, g, v = place(2 * k)
            if kind == "r":
                src = w_res[m, 512 * g : 512 * (g + 1), :]
            else:
                src = w_head[m, 512 * g : 512 * (g + 1), 512 * v : 512 * v + 1024]
            src = src.rearrange("(p j) c -> p j c", j=J)
            if k == 0:
                for part in range(2):
                    cols = slice(512 * part, 512 * (part + 1))
                    nc.sync.dma_start(out=raw[:, :, cols], in_=src[:, :, cols])
            else:
                nc.sync.dma_start(out=raw[:], in_=src)
            raw_tiles[k] = raw

        def copy_on(scalar, out, in_):
            if scalar:
                nc.scalar.copy(out=out, in_=in_)
            else:
                nc.vector.tensor_copy(out=out, in_=in_)

        used = []

        def interleave(c):
            k, part = divmod(c, 2)
            mid = mids.tile([P, 2048], BF16, name="mid", align_bytes=64)
            src = raw_tiles[k][:, :, 512 * part : 512 * (part + 1)]
            if c < RES_CHUNKS:
                dv = mid[:].rearrange("p (t m j) -> p m j t", t=4, j=4)
                sv = src.rearrange("p j (m t) -> p m j t", t=4)
                on_scalar = c in S_RES
            else:
                dv = mid[:].rearrange("p (c i j) -> p c j i", i=4, j=4)
                sv = src.rearrange("p j (c i) -> p c j i", i=4)
                on_scalar = (c - RES_CHUNKS) % 8 in S_HEAD or c in S_EXTRA
            copy_on(on_scalar, dv, sv)
            mid_tiles[c] = mid
            used.append(k)
            if used.count(k) == 2:
                load(k + RAW_BUFS)

        def quantize(c):
            cw = codes.tile([P, 512], U32, name="cw", align_bytes=64)
            cs = codes.tile([P, 512], U8, name="cs", align_bytes=64)
            nc.vector.quantize_mx(out=cw[:].bitcast(FP8X4), scales=cs[:], in_=mid_tiles[c][:])
            code_tiles[place(c)] = (cw, cs)

        par = const.tile([P, 512], BF16, name="par")
        nc.vector.memset(par[:], 0.0)
        warm = const.tile([P, 2], F32, name="warm")
        nc.vector.memset(warm[:], 0.0)
        load(0)
        nc.sync.dma_start(out=par[0:6, :], in_=a_skip.rearrange("m (g c) -> (m g) c", g=2))
        nc.sync.dma_start(out=par[6:12, :], in_=g_silu.rearrange("m (g c) -> (m g) c", g=2))
        nc.sync.dma_start(out=par[12:14, 0:128], in_=temp.rearrange("(i p) -> i p", p=P))
        h_sb = work.tile([P, 2, 1024], BF16, name="big", bufs=3, align_bytes=64)
        nc.sync.dma_start(out=h_sb[:], in_=h.rearrange("(i p) k -> p i k", p=P))
        for k in range(1, RAW_BUFS):
            load(k)
        nc.scalar.activation(out=warm[:, 1:2], in_=warm[:, 0:1], func=ACT.Silu)

        ident_f = const.tile([P, P], F32, name="ident_f")
        make_identity(nc, ident_f[:])
        ident_b = const.tile([P, P], BF16, name="ident_b")
        nc.vector.tensor_copy(out=ident_b[:], in_=ident_f[:])
        half_t = const.tile([P, 2], F32, name="half_t")
        nc.gpsimd.memset(half_t[:], 0.5)
        two_t = const.tile([P, 2], F32, name="two_t")
        nc.gpsimd.memset(two_t[:], 2.0)

        pcol = const.tile([P, 5, 16], F32, name="pcol")
        s2 = const.tile([P, 2], F32, name="s2")

        def params():
            par_t = pt.tile([P, 5, P], BF16, name="tp")
            for t in range(4):
                nc.tensor.transpose(par_t[:, t, :], par[:, t::4], ident_b[:])
            nc.tensor.transpose(par_t[:, 4, :], par[:, 0:P], ident_b[:])
            nc.vector.tensor_copy(out=pcol[:], in_=par_t[:, :, 0:16])

        def scales2():
            nc.vector.reciprocal(out=s2[:], in_=pcol[:, 4, 12:14])
            nc.vector.tensor_scalar(out=s2[:], in0=s2[:], scalar1=0.5, scalar2=None, op0=ALU.mult)

        diag_a = const.tile([P, 24, P], BF16, name="diag_a")
        diag_g = const.tile([P, 24, P], F32, name="diag_g")

        def diags(m, g, t, scalar):
            if True:
                if True:
                    x = (2 * m + g) * 4 + t
                    col = 2 * m + g
                    for dst, ident, off in ((diag_a, ident_b, 0), (diag_g, ident_f, 6)):
                        fac = pcol[:, t, off + col : off + col + 1]
                        if scalar:
                            nc.scalar.activation(out=dst[:, x, :], in_=ident[:], func=ACT.Copy, scale=fac)
                        else:
                            nc.vector.tensor_scalar(out=dst[:, x, :], in0=ident[:], scalar1=fac, scalar2=None, op0=ALU.mult)

        hT, hq, hs = [], [], []

        def prepare_h(g):
            h_words = h_sb[:].rearrange("p i k -> p (i k)").bitcast(F32)
            tp = pt.tile([P, 2, 2, P], F32, name="tp")
            for i in range(2):
                for u in range(2):
                    base = 512 * i + 256 * g
                    nc.tensor.transpose(tp[:, i, u, :], h_words[:, base + u : base + 256 : 2], ident_f[:])
            hx = const.tile([P, N, 4], BF16, name="hT%d" % g, align_bytes=64)
            copy_on(
                H_SCALAR,
                out=hx[:].rearrange("p n t -> p (n t)").bitcast(F32).rearrange("p (i n u) -> p i n u", i=2, u=2),
                in_=tp[:].rearrange("p i u n -> p i n u"),
            )
            hT.append(hx)

        def quantize_h(g):
            qc = const.tile([P, N], U32, name="hq%d" % g, align_bytes=64)
            qs = const.tile([P, N], U8, name="hs%d" % g, align_bytes=64)
            nc.vector.quantize_mx(out=qc[:].bitcast(FP8X4), scales=qs[:], in_=hT[g][:].rearrange("p n t -> p (n t)"))
            hq.append(qc)
            hs.append(qs)

        silu_tiles, r_mids, r_codes = {}, {}, {}

        u_banks = {}

        def stage1(m, g, tt):
            if True:
                if True:
                    bank = pm.tile([P, 2, N], F32, name="mm")
                    for t2 in range(2):
                        t = 2 * tt + t2
                        for kp in range(2):
                            cw, cs = code_tiles["r", m, kp, g]
                            nc.tensor.matmul_mx(
                                out=bank[:, t2, :],
                                lhsT=cw[:, P * t : P * (t + 1)].bitcast(FP8X4),
                                lhsT_scale=cs[:, P * t : P * (t + 1)],
                                rhs=hq[kp][:].bitcast(FP8X4),
                                rhs_scale=hs[kp][:],
                                start=(kp == 0),
                                stop=(kp == 1),
                            )
                    u_banks[m, g, tt] = bank

        def silu(m, g, tt):
            if tt == 0:
                sl = work.tile([P, 4, N], F32, name="big", bufs=3, align_bytes=64)
                silu_tiles[m, g] = sl
            sl = silu_tiles[m, g]
            nc.scalar.activation(out=sl[:, 2 * tt : 2 * tt + 2, :], in_=u_banks[m, g, tt][:], func=ACT.Silu)

        r_banks = {}

        def mix(m, g, i):
            sl = silu_tiles[m, g]
            if True:
                bank = pt.tile([P, 4, P], F32, name="tp")
                tok = slice(P * i, P * (i + 1))
                for t in range(4):
                    x = (2 * m + g) * 4 + t
                    nc.tensor.matmul(bank[:, t, :], lhsT=diag_a[:, x, :], rhs=hT[g][:, tok, t], start=True, stop=False)
                    nc.tensor.matmul(bank[:, t, :], lhsT=diag_g[:, x, :], rhs=sl[:, t, tok], start=False, stop=True)
                r_banks[m, g, i] = bank

        def mix_out(m, g, i):
            if i == 0:
                rb = work.tile([P, N, 4], BF16, name="rb", align_bytes=64)
                r_mids[m, g] = rb
            copy_on(True, r_mids[m, g][:, P * i : P * (i + 1), :], r_banks[m, g, i][:].rearrange("p t n -> p n t"))

        def quantize_r(m, g):
            if g == 0:
                rc = const.tile([P, 2, N], U32, name="rc%d" % m, align_bytes=64)
                rs = const.tile([P, 2, N], U8, name="rs%d" % m, align_bytes=64)
                r_codes[m] = (rc, rs)
            rc, rs = r_codes[m]
            nc.vector.quantize_mx(out=rc[:, g, :].bitcast(FP8X4), scales=rs[:, g, :], in_=r_mids[m, g][:].rearrange("p n t -> p (n t)"))

        mx = const.tile([P, 24], F32, name="mx")
        ms = const.tile([P, 6], F32, name="ms")
        nms = const.tile([P, 6], F32, name="nms")
        z_tiles, q_tiles, w_tiles, z_banks = {}, {}, {}, {}
        sums = {}

        def logits(m, v, i):
            if True:
                bank = pm.tile([P, 512], F32, name="mm")
                rc, rs = r_codes[m]
                for g in range(2):
                    cw, cs = code_tiles["h", m, g, v]
                    nc.tensor.matmul_mx(
                        out=bank[:],
                        lhsT=rc[:, g, P * i : P * (i + 1)].bitcast(FP8X4),
                        lhsT_scale=rs[:, g, P * i : P * (i + 1)],
                        rhs=cw[:].bitcast(FP8X4),
                        rhs_scale=cs[:],
                        start=(g == 0),
                        stop=(g == 1),
                    )
                z_banks[2 * m + i, v] = bank

        def scale_max(m, v, i):
            u = 2 * m + i
            if v == 0:
                zs = units.tile([P, V], F32, name="zs")
                z_tiles[u] = zs
            nc.vector.tensor_scalar(
                out=z_tiles[u][:, 512 * v : 512 * (v + 1)], in0=z_banks[u, v][:], scalar1=s2[:, i : i + 1], scalar2=None,
                op0=ALU.mult, op1=ALU.max, accum_out=mx[:, 4 * u + v : 4 * u + v + 1],
            )

        def row_max(m):
            us = slice(2 * m, 2 * m + 2)
            nc.vector.tensor_reduce(out=ms[:, us], in_=mx[:, 8 * m : 8 * m + 8].rearrange("p (i v) -> p i v", v=4), axis=mybir.AxisListType.X, op=ALU.max)
            nc.vector.tensor_scalar(out=nms[:, us], in0=ms[:, us], scalar1=-1.0, scalar2=None, op0=ALU.mult)

        for m in range(HEADS):
            ss = const.tile([P, 2], F32, name="ss%d" % m)
            ts = const.tile([P, 2], F32, name="ts%d" % m)
            sums[m] = (ss, ts)

        def expo(u):
            if u < 4:
                q = units.tile([P, V], F32, name="q", bufs=4)
            else:
                q = raws.tile([P, V], F32, name="raw")
            q_tiles[u] = q
            nc.scalar.activation(out=q[:], in_=z_tiles[u][:], func=ACT.Exp, bias=nms[:, u : u + 1], scale=1.0)

        def square(u):
            w = work.tile([P, V], F32, name="w", bufs=1)
            w_tiles[u] = w
            m, i = divmod(u, 2)
            q = q_tiles[u]
            acc = sums[m][0][:, i : i + 1]
            if u in V_SQUARES:
                nc.vector.scalar_tensor_tensor(out=w[:], in0=q[:], scalar=1.0, in1=q[:], op0=ALU.mult, op1=ALU.mult, accum_out=acc)
            else:
                nc.scalar.activation(out=w[:], in_=q[:], func=ACT.Square, accum_out=acc)

        def tpass(u):
            w = w_tiles[u]
            m, i = divmod(u, 2)
            nc.vector.scalar_tensor_tensor(
                out=w[:], in0=z_tiles[u][:], scalar=ms[:, u : u + 1], in1=w[:], op0=ALU.subtract, op1=ALU.mult,
                accum_out=sums[m][1][:, i : i + 1],
            )

        kappas = {}

        def kappa(m):
            ss, ts = sums[m]
            root = const.tile([P, 2], F32, name="root%d" % m)
            rec = const.tile([P, 2], F32, name="rec%d" % m)
            ex = const.tile([P, 2], F32, name="ex%d" % m)
            pw = const.tile([P, 2], F32, name="pw%d" % m)
            lim = const.tile([P, 2], F32, name="lim%d" % m)
            kap = const.tile([P, 2], F32, name="kap%d" % m)
            kappas[m] = kap
            nc.gpsimd.tensor_tensor(out=root[:], in0=ss[:], in1=half_t[:], op=ALU.pow)
            nc.vector.reciprocal(out=rec[:], in_=ss[:])
            nc.vector.scalar_tensor_tensor(out=ex[:], in0=ts[:], scalar=1.0 / math.log(2.0), in1=rec[:], op0=ALU.mult, op1=ALU.mult)
            nc.gpsimd.tensor_tensor(out=pw[:], in0=two_t[:], in1=ex[:], op=ALU.pow)
            nc.gpsimd.tensor_scalar(out=lim[:], in0=root[:], scalar1=math.sqrt(EPS), scalar2=0.0, op0=ALU.mult, op1=ALU.add)
            nc.gpsimd.tensor_scalar(out=pw[:], in0=pw[:], scalar1=math.sqrt(DELTA), scalar2=0.0, op0=ALU.mult, op1=ALU.add)
            nc.vector.tensor_tensor(out=kap[:], in0=pw[:], in1=lim[:], op=ALU.min)

        def ln(u, q4=None):
            cols = slice(0, V) if q4 is None else slice(512 * q4, 512 * (q4 + 1))
            m, i = divmod(u, 2)
            q = q_tiles[u]
            nc.scalar.activation(out=q[:, cols], in_=q[:, cols], func=ACT.Ln, bias=kappas[m][:, i : i + 1], scale=1.0)

        def final(u, q4=None):
            cols = slice(0, V) if q4 is None else slice(512 * q4, 512 * (q4 + 1))
            m, i = divmod(u, 2)
            z = z_tiles[u]
            nc.vector.scalar_tensor_tensor(out=z[:, cols], in0=z[:, cols], scalar=ms[:, u : u + 1], in1=q_tiles[u][:, cols], op0=ALU.subtract, op1=ALU.subtract)
            nc.sync.dma_start(out=out_0[m, P * i : P * (i + 1), cols], in_=z[:, cols])

        p_mids = {}

        t_banks = {}

        def turn(u, g):
            z = z_tiles[u]
            bank = (pm if g % 2 else pt).tile([P, 4, P], F32, name="mm" if g % 2 else "tp")
            for t in range(4):
                nc.tensor.transpose(bank[:, t, :], z[:, 512 * g + t : 512 * (g + 1) : 4], ident_f[:])
            t_banks[u, g] = bank

        def turn_out(u, g, scalar):
            if u not in p_mids:
                pb = work.tile([P, 4, P, 4], BF16, name="big", bufs=3, align_bytes=64)
                p_mids[u] = pb
            copy_on(scalar, p_mids[u][:, g, :, :], t_banks[u, g][:].rearrange("p t n -> p n t"))

        p_codes = {}

        def planes(u, group=None):
            gs = slice(0, 4) if group is None else slice(group, group + 1)
            if group in (None, 0):
                pc = work.tile([P, 4, P], U32, name="pc", align_bytes=64, bufs=PB)
                ps = work.tile([P, 4, P], U8, name="ps", align_bytes=64, bufs=PB)
                p_codes[u] = (pc, ps)
            pc, ps = p_codes[u]
            nc.vector.quantize_mx(
                out=pc[:, gs, :].rearrange("p g n -> p (g n)").bitcast(FP8X4),
                scales=ps[:, gs, :].rearrange("p g n -> p (g n)"),
                in_=p_mids[u][:, gs, :, :].rearrange("p g n t -> p (g n t)"),
            )
            nc.sync.dma_start(out=words[:, gs, P * u : P * (u + 1)], in_=pc[:, gs, :].bitcast(I32))
            if group in (None, 3):
                for q4 in range(4):
                    nc.sync.dma_start(
                        out=scale_rows[:, 4 * q4 : 4 * q4 + 4, 32 * u : 32 * (u + 1)].rearrange("g r m -> r g m"),
                        in_=ps[32 * q4 : 32 * q4 + 4, :, :].bitcast(I32),
                    )

        steps = {"interleave": interleave, "quantize": quantize, "params": params, "scales2": scales2, "diags": diags, "prepare_h": prepare_h, "quantize_h": quantize_h, "stage1": stage1, "silu": silu, "mix": mix, "mix_out": mix_out, "quantize_r": quantize_r, "logits": logits, "scale_max": scale_max, "row_max": row_max, "expo": expo, "square": square, "tpass": tpass, "kappa": kappa, "ln": ln, "final": final, "turn": turn, "turn_out": turn_out, "planes": planes}
        for name, args in ORDER:
            steps[name](*args)
